import numpy as np
import ml_dtypes


def mxq(x, axis, fmt="e4m3"):
    dtype, down = {"e4m3": (ml_dtypes.float8_e4m3fn, 7), "e5m2": (ml_dtypes.float8_e5m2, 14)}[fmt]
    v = np.moveaxis(np.asarray(x, np.float32).astype(ml_dtypes.bfloat16).astype(np.float64), axis, -1)
    blocks = v.reshape(v.shape[:-1] + (-1, 32))
    amax = np.abs(blocks).max(-1, keepdims=True)
    byte = np.maximum(np.where(amax > 0, np.frexp(amax)[1] - 1 + 127, 0) - down, 1)
    scale = np.exp2(byte - 127.0)
    codes = (blocks / scale).astype(np.float32).astype(dtype).astype(np.float64)
    return np.moveaxis((codes * scale).reshape(v.shape), -1, axis)


WIDE = False


def mx_kscale(k):
    if not WIDE:
        return np.ones(k)
    levels = np.array([10, -10, 5, -5, 0])
    if k % 512:
        return np.exp2(np.random.permutation(np.resize(levels, k // 32))).repeat(32)
    a = np.empty((k // 512, 16))
    for p in range(k // 512):
        a[p, :8] = np.random.permutation(np.resize(levels, 8))
        for g in range(8):
            far = levels[np.abs(levels - a[p, g]) >= 10]
            a[p, g + 8] = far[np.random.randint(len(far))]
    return np.exp2(a.ravel()).repeat(32)


def f64(x):
    return np.asarray(x).astype(np.float64)


def striped(idx):
    return np.tile(idx.reshape(-1, 16).T, (8, 1)).astype(np.uint16)


def unstriped(offs):
    return offs[:16].T.reshape(-1).astype(np.int64)


E2M1 = np.array([0.0, 0.5, 1.0, 1.5, 2.0, 3.0, 4.0, 6.0, -0.0, -0.5, -1.0, -1.5, -2.0, -3.0, -4.0, -6.0])


def pack_weight(w, fmt):
    k, n = w.shape
    w = f64(np.asarray(w, np.float32).astype(ml_dtypes.bfloat16)).reshape(k // 32, 32, n)
    amax = np.abs(w).max(1)
    if fmt == "e4m3":
        byte = np.frexp(amax)[1] - 1 + 127 - 7
    else:
        mant, ex = np.frexp(amax / 6.0)
        byte = np.where(mant > 0.5, ex, ex - 1) + 127
    byte = np.clip(np.where(amax > 0, byte, 1), 1, 254)
    scaled = (w * np.exp2(127.0 - byte)[:, None, :]).reshape(k, n).astype(np.float32)
    by_word = np.ascontiguousarray(scaled.reshape(k // 512, 128, 4, n).transpose(0, 1, 3, 2))
    if fmt == "e4m3":
        words = by_word.astype(ml_dtypes.float8_e4m3fn).view(np.uint8)
    else:
        c = by_word.astype(ml_dtypes.float4_e2m1fn).view(np.uint8) & 0xF
        words = (c[..., 0::2] | (c[..., 1::2] << 4)).reshape(k // 512, 128, 2 * n)
    return np.ascontiguousarray(words), np.ascontiguousarray(byte.astype(np.uint8).reshape(k // 512, 16, n))


def unpack_weight(words, scales, fmt):
    g, _, n = scales.shape
    words = np.ascontiguousarray(words).reshape(g, 128, n, -1)
    if fmt == "e4m3":
        vals = words.view(ml_dtypes.float8_e4m3fn).astype(np.float64)
    else:
        nib = np.empty((g, 128, n, 4), np.uint8)
        nib[..., 0::2] = words & 0xF
        nib[..., 1::2] = words >> 4
        vals = E2M1[nib]
    vals = vals * np.repeat(np.exp2(scales.astype(np.float64) - 127.0), 8, axis=1)[..., None]
    return vals.transpose(0, 1, 3, 2).reshape(g * 512, n)


def gelu(v):
    return 0.5 * v * (1.0 + np.tanh(np.sqrt(2.0 / np.pi) * (v + 0.044715 * v**3)))


def bf(x):
    return np.asarray(x, np.float32).astype(ml_dtypes.bfloat16)


def planes(Y):
    n, m = Y.shape
    b = f64(bf(Y)).reshape(n // 32, 32, m)
    amax = np.abs(b).max(1)
    byte = np.clip(np.where(amax > 0, np.frexp(amax)[1] - 1 + 127 - 7, 1), 1, 254)
    codes = (b * np.exp2(127.0 - byte)[:, None, :]).reshape(n, m).astype(np.float32).astype(ml_dtypes.float8_e4m3fn).view(np.uint8)
    words = codes.reshape(n // 512, 128, 4, m).transpose(0, 1, 3, 2)
    return np.ascontiguousarray(words), np.ascontiguousarray(byte.astype(np.uint8).reshape(n // 512, 16, m))


K, H, N, T, S, T2, P = 1536, 512, 384, 4096, 1024, 2048, 1024

def setup_inputs():
    n = np.random.standard_normal
    s = mx_kscale(K)[:, None]
    u = mx_kscale(H)[:, None]
    d = {}
    d["tab_words"], d["tab_scales"] = pack_weight(n((K, T)) * s, "e4m3")
    d["offs"] = striped(np.random.permutation(T)[:S])
    d["w1"] = (n((K, H)) / K**0.5 / s).astype(np.float32)
    d["w4_words"], d["w4_scales"] = pack_weight(n((K, H)) / K**0.5 / s, "e2m1")
    d["gain"] = (0.6 * np.exp(0.3 * n(H)) * u[:, 0]).astype(np.float32)
    d["wgs"] = np.exp(0.3 * n((128, S))).astype(np.float32)
    d["page0"] = (n((H, T2)) * u).astype(np.float32)
    d["offs2"] = striped(np.random.permutation(T2)[:S])
    d["offs3"] = striped(np.random.permutation(T2)[:P])
    d["bias"] = (0.8 * n(H) * u[:, 0]).astype(np.float32)
    d["w2"] = (n((H, N)) / H**0.5 / u).astype(np.float32)
    return d

def reference(tab_words, tab_scales, offs, w1, w4_words, w4_scales, gain, wgs, page0, offs2, offs3, bias, w2):
    v = unpack_weight(tab_words, tab_scales, "e4m3")[:, unstriped(offs)]
    w4 = unpack_weight(w4_words, w4_scales, "e2m1")
    a = mxq(f64(w1), 0, "e4m3").T @ v
    b = w4.T @ v
    h = f64(gain)[:, None] * (a * b + a + b)
    page = f64(page0).copy()
    page[:, unstriped(offs2)] = np.tile(f64(wgs), (H // 128, 1)) * h
    x = page[:, unstriped(offs3)] + f64(bias)[:, None]
    y = mxq(f64(w2), 0, "e4m3").T @ mxq(x, 0, "e4m3")
    words, scales = planes(page)
    return y, page, words, scales

@@ -1,0 +1,320 @@
+from contextlib import ExitStack
+
+import concourse.mybir as mybir
+from concourse.masks import make_identity
+
+K, H, N, T, S, T2, M = 1536, 512, 384, 4096, 1024, 2048, 1024
+FLOPS = 2 * (2 * K * H * S + H * N * M)
+
+F32 = mybir.dt.float32
+BF16 = mybir.dt.bfloat16
+I32 = mybir.dt.int32
+U32 = mybir.dt.uint32
+U16 = mybir.dt.uint16
+U8 = mybir.dt.uint8
+FP8X4 = mybir.dt.float8_e4m3fn_x4
+FP4X4 = mybir.dt.float4_e2m1fn_x4
+ADD = mybir.AluOpType.add
+MULT = mybir.AluOpType.mult
+IDENTITY = mybir.ActivationFunctionType.Identity
+
+P = 128
+PACK = 4
+PASSES = K // (P * PACK)
+BANK = 512
+BLOCKS = S // P
+LANE = 16
+
+
+def tile_list_broodstock_spawning_board_kernel(
+    tc, tab_words, tab_scales, offs, w1, w4_words, w4_scales, gain, wgs, page0, offs2, offs3, bias, w2,
+    out_0, out_1, out_2, out_3,
+):
+    nc = tc.nc
+    with ExitStack() as ctx:
+        lists = ctx.enter_context(tc.tile_pool(name="lists", bufs=1))
+        keep = ctx.enter_context(tc.tile_pool(name="keep", bufs=1))
+        share = ctx.enter_context(tc.tile_pool(name="share", bufs=1))
+        psum = ctx.enter_context(tc.psum_pool(name="psum", bufs=1))
+
+        def small(shape, dtype, name):
+            return share.tile(shape, dtype, name=name, tag="small", bufs=6, align_bytes=64)
+
+        def medium(shape, dtype, name):
+            return share.tile(shape, dtype, name=name, tag="medium", bufs=2, align_bytes=64)
+
+        def large(shape, dtype, name):
+            return share.tile(shape, dtype, name=name, tag="large", bufs=2, align_bytes=64)
+
+        def bank(index, name):
+            return psum.tile([P, BANK], F32, name=name, tag="bank%d" % index)
+
+        scale_rows = keep.tile([P, T], U8, name="scale_rows", align_bytes=64)
+        nc.vector.memset(scale_rows[:].bitcast(I32), 0)
+        nc.gpsimd.dma_start(
+            out=scale_rows[0 : PASSES * 16, :].bitcast(I32),
+            in_=tab_scales.rearrange("a q t -> (a q) t").bitcast(I32),
+        )
+        w4_plane = keep.tile([P, PASSES, H], U8, name="w4_plane", align_bytes=64)
+        nc.vector.memset(w4_plane[:].rearrange("p a c -> p (a c)").bitcast(I32), 0)
+        v_plane = keep.tile([P, PASSES, S], U8, name="v_plane", align_bytes=64)
+        nc.vector.memset(v_plane[:].rearrange("p a c -> p (a c)").bitcast(I32), 0)
+        for q in range(4):
+            nc.gpsimd.dma_start(
+                out=w4_plane[32 * q : 32 * q + 4, :, :].bitcast(I32),
+                in_=w4_scales[:, 4 * q : 4 * q + 4, :].rearrange("a r c -> r a c").bitcast(I32),
+            )
+
+        gain_col = keep.tile([P, PACK], F32, name="gain_col")
+        nc.gpsimd.dma_start(out=gain_col[:], in_=gain.rearrange("(p t) -> p t", t=PACK))
+        bias_col = keep.tile([P, PACK], F32, name="bias_col")
+        nc.gpsimd.dma_start(out=bias_col[:], in_=bias.rearrange("(p t) -> p t", t=PACK))
+        ident = keep.tile([P, P], F32, name="ident")
+        make_identity(nc, ident[:])
+
+        idx = lists.tile([P, S // LANE], U16, name="idx")
+        nc.sync.dma_start(idx[:], offs)
+        table = []
+        w4_codes = keep.tile([P, PASSES, 2 * H], U8, name="w4_codes", align_bytes=64)
+        for a in range(PASSES):
+            words = keep.tile([P, T], U32, name="table%d" % a, align_bytes=64)
+            nc.sync.dma_start(
+                out=words[:].bitcast(I32), in_=tab_words[a].rearrange("p t i -> p (t i)").bitcast(I32)
+            )
+            table.append(words)
+            if a == 0:
+                nc.sync.dma_start(
+                    out=w4_codes[:].bitcast(I32), in_=w4_words.rearrange("a p c -> p a c").bitcast(I32)
+                )
+        w1_pieces = [(0, 0, H), (1, 0, H), (2, 0, H // 2), (2, H // 2, H)]
+        w1_raw = []
+        for a, c0, c1 in w1_pieces:
+            alloc = medium if c1 - c0 == H else small
+            raw = alloc([P, PACK, c1 - c0], F32, "w1_raw")
+            rows = w1[512 * a : 512 * (a + 1), c0:c1].rearrange("(p j) c -> p j c", j=PACK)
+            nc.sync.dma_start(out=raw[:], in_=rows)
+            w1_raw.append(raw)
+        idx2 = lists.tile([P, S // LANE], U16, name="idx2")
+        nc.sync.dma_start(idx2[:], offs2)
+        page, wgs_rows = [], []
+        page_src = page0.rearrange("(p t) c -> t p c", t=PACK)
+        wgs_src = wgs.rearrange("(s t) j -> t s j", t=PACK)
+        for t in range(PACK):
+            board = keep.tile([P, T2], F32, name="page%d" % t, align_bytes=64)
+            nc.sync.dma_start(out=board[:], in_=page_src[t])
+            page.append(board)
+            factor = keep.tile([P, S], F32, name="wgs%d" % t, align_bytes=64)
+            for q in (0, 2, 1, 3):
+                nc.sync.dma_start(out=factor[32 * q : 32 * (q + 1), :], in_=wgs_src[t])
+            wgs_rows.append(factor)
+            if t == 0:
+                idx3 = lists.tile([P, M // LANE], U16, name="idx3")
+                nc.sync.dma_start(idx3[:], offs3)
+
+        picked_rows = keep.tile([P, S], U8, name="picked_rows", align_bytes=64)
+        nc.vector.tensor_copy(picked_rows[:], scale_rows[:].indirect(idx[:]))
+        for a in range(PASSES):
+            for q in range(4):
+                r0 = 16 * a + 4 * q
+                nc.gpsimd.dma_start(
+                    out=v_plane[32 * q : 32 * q + 4, a, :].bitcast(I32),
+                    in_=picked_rows[r0 : r0 + 4, :].bitcast(I32),
+                )
+
+        v_codes = []
+        for a in range(PASSES):
+            picked = keep.tile([P, S], U32, name="v_codes%d" % a, align_bytes=64)
+            if a < PASSES - 1:
+                nc.vector.tensor_copy(picked[:], table[a][:].indirect(idx[:]))
+            else:
+                for half in range(2):
+                    nc.vector.tensor_copy(
+                        picked[:, half * BANK : (half + 1) * BANK],
+                        table[a][:].indirect(idx[:, half * 32 : (half + 1) * 32]),
+                    )
+            v_codes.append(picked)
+
+        b_banks = [bank(j, "b_bank") for j in range(BLOCKS)]
+        for a in range(PASSES):
+            for j in range(BLOCKS):
+                cols = slice(j * P, (j + 1) * P)
+                nc.tensor.matmul_mx(
+                    out=b_banks[j][:],
+                    lhsT=v_codes[a][:, cols].bitcast(FP8X4),
+                    lhsT_scale=v_plane[:, a, cols],
+                    rhs=w4_codes[:, a, :].bitcast(FP4X4),
+                    rhs_scale=w4_plane[:, a, :],
+                    start=(a == 0),
+                    stop=(a == PASSES - 1),
+                )
+        b_sb = large([P, BLOCKS, H], F32, "b_sb")
+        for j in range(BLOCKS):
+            nc.scalar.activation(
+                out=b_sb[:, j, :].rearrange("p (t m) -> p t m", t=PACK),
+                in_=b_banks[j][:].rearrange("p (m t) -> p t m", t=PACK),
+                func=IDENTITY,
+            )
+
+        w1_codes, w1_plane = [], []
+        for (a, c0, c1), raw in zip(w1_pieces, w1_raw):
+            width = c1 - c0
+            grouped = small([P, width, PACK], BF16, "w1_grouped")
+            nc.vector.tensor_copy(
+                out=grouped[:].rearrange("p (c i) j -> p c j i", i=4),
+                in_=raw[:].rearrange("p j (c i) -> p c j i", i=4),
+            )
+            codes = keep.tile([P, width], U32, name="w1_codes%d_%d" % (a, c0), align_bytes=64)
+            plane = keep.tile([P, width], U8, name="w1_plane%d_%d" % (a, c0), align_bytes=64)
+            nc.vector.quantize_mx(
+                out=codes[:].bitcast(FP8X4), scales=plane[:], in_=grouped[:].rearrange("p c j -> p (c j)")
+            )
+            w1_codes.append(codes)
+            w1_plane.append(plane)
+
+        a_banks = [bank(j, "a_bank") for j in range(BLOCKS)]
+
+        def a_pass(j, piece):
+            a, c0, c1 = w1_pieces[piece]
+            cols = slice(j * P, (j + 1) * P)
+            nc.tensor.matmul_mx(
+                out=a_banks[j][:, c0:c1],
+                lhsT=v_codes[a][:, cols].bitcast(FP8X4),
+                lhsT_scale=v_plane[:, a, cols],
+                rhs=w1_codes[piece][:].bitcast(FP8X4),
+                rhs_scale=w1_plane[piece][:],
+                start=(piece == 0),
+                stop=(piece == len(w1_pieces) - 1),
+            )
+
+        for piece in range(2):
+            for j in range(BLOCKS):
+                a_pass(j, piece)
+        for j in range(BLOCKS):
+            a_pass(j, 2)
+            a_pass(j, 3)
+
+        u_sb = large([P, BLOCKS, H], F32, "u_sb")
+        for j in range(BLOCKS):
+            nc.vector.scalar_tensor_tensor(
+                out=u_sb[:, j, :].rearrange("p (t m) -> p t m", t=PACK),
+                in0=b_sb[:, j, :].rearrange("p (t m) -> p t m", t=PACK),
+                scalar=1.0,
+                in1=a_banks[j][:].rearrange("p (m t) -> p t m", t=PACK),
+                op0=ADD,
+                op1=MULT,
+            )
+
+        h = [small([P, S], F32, "h") for t in range(PACK)]
+        for half in range(2):
+            for t in range(PACK):
+                acc = bank(4 * half + t, "h_bank")
+                for jj in range(4):
+                    j = 4 * half + jj
+                    for first, src in ((True, u_sb), (False, b_sb)):
+                        nc.tensor.matmul(
+                            acc[:, jj * P : (jj + 1) * P],
+                            src[:, j, t * P : (t + 1) * P],
+                            ident[:],
+                            start=first,
+                            stop=not first,
+                            is_transpose=True,
+                        )
+                nc.scalar.activation(
+                    out=h[t][:, half * BANK : (half + 1) * BANK],
+                    in_=acc[:],
+                    func=IDENTITY,
+                    scale=gain_col[:, t : t + 1],
+                )
+
+        w2_raw = medium([P, PACK, N], F32, "w2_raw")
+        nc.sync.dma_start(out=w2_raw[:], in_=w2.rearrange("(p j) n -> p j n", j=PACK))
+
+        out1_dst = out_1.rearrange("(p t) c -> t p c", t=PACK)
+        page_bf = large([P, PACK, T2], BF16, "page_bf")
+        page_grouped = large([P, T2, PACK], BF16, "page_grouped")
+        x_grouped = medium([P, M, PACK], BF16, "x_grouped")
+        w2_grouped = keep.tile([P, N, PACK], BF16, name="w2_grouped", align_bytes=64)
+        w2_codes = keep.tile([P, N], U32, name="w2_codes", align_bytes=64)
+        w2_plane = keep.tile([P, N], U8, name="w2_plane", align_bytes=64)
+
+        def pieces(count, total):
+            step = total // count
+            return [(i * step, (i + 1) * step) for i in range(count)]
+
+        for t in range(PACK):
+            last = t == PACK - 1
+            for c0, c1 in pieces(2 if t == 0 else 1, S):
+                nc.vector.tensor_tensor(
+                    page[t][:].indirect(idx2[:, c0 // LANE : c1 // LANE]),
+                    h[t][:, c0:c1],
+                    wgs_rows[t][:, c0:c1],
+                    MULT,
+                )
+            nc.sync.dma_start(out=out1_dst[t], in_=page[t][:])
+            picked = small([P, M], F32, "picked")
+            for c0, c1 in pieces(2 if last else 1, T2):
+                nc.scalar.copy(out=page_bf[:, t, c0:c1], in_=page[t][:, c0:c1])
+            for c0, c1 in pieces(2 if last else 1, M):
+                nc.vector.tensor_copy(picked[:, c0:c1], page[t][:].indirect(idx3[:, c0 // LANE : c1 // LANE]))
+                nc.scalar.activation(
+                    out=x_grouped[:, c0:c1, t],
+                    in_=picked[:, c0:c1],
+                    func=IDENTITY,
+                    bias=bias_col[:, t : t + 1],
+                )
+            if t == 0:
+                nc.scalar.copy(
+                    out=w2_grouped[:].rearrange("p (c i) j -> p c j i", i=4),
+                    in_=w2_raw[:].rearrange("p j (c i) -> p c j i", i=4),
+                )
+            if t == 1:
+                nc.scalar.copy(out=page_grouped[:, :, 0:2], in_=page_bf[:, 0:2, :].rearrange("p t m -> p m t"))
+                for c0, c1 in ((0, 256), (256, N)):
+                    nc.vector.quantize_mx(
+                        out=w2_codes[:, c0:c1].bitcast(FP8X4),
+                        scales=w2_plane[:, c0:c1],
+                        in_=w2_grouped[:, c0:c1, :].rearrange("p c j -> p (c j)"),
+                    )
+
+        page_codes = keep.tile([P, T2], U32, name="page_codes", align_bytes=64)
+        page_plane = keep.tile([P, T2], U8, name="page_plane", align_bytes=64)
+        x_codes = keep.tile([P, M], U32, name="x_codes", align_bytes=64)
+        x_plane = keep.tile([P, M], U8, name="x_plane", align_bytes=64)
+        out2_dst = out_2[0].rearrange("p m t -> p (m t)").bitcast(I32)
+        for half in range(2):
+            pc = slice(half * T2 // 2, (half + 1) * T2 // 2)
+            xc = slice(half * BANK, (half + 1) * BANK)
+            nc.vector.tensor_copy(
+                out=page_grouped[:, pc, 2:4], in_=page_bf[:, 2:4, pc].rearrange("p t m -> p m t")
+            )
+            nc.vector.quantize_mx(
+                out=x_codes[:, xc].bitcast(FP8X4),
+                scales=x_plane[:, xc],
+                in_=x_grouped[:, xc, :].rearrange("p c j -> p (c j)"),
+            )
+            nc.vector.quantize_mx(
+                out=page_codes[:, pc].bitcast(FP8X4),
+                scales=page_plane[:, pc],
+                in_=page_grouped[:, pc, :].rearrange("p c j -> p (c j)"),
+            )
+            for n in range(N // P):
+                rows = slice(n * P, (n + 1) * P)
+                acc = bank(3 * half + n, "y_bank")
+                nc.tensor.matmul_mx(
+                    out=acc[:],
+                    lhsT=w2_codes[:, rows].bitcast(FP8X4),
+                    lhsT_scale=w2_plane[:, rows],
+                    rhs=x_codes[:, xc].bitcast(FP8X4),
+                    rhs_scale=x_plane[:, xc],
+                    start=True,
+                    stop=True,
+                )
+                y = small([P, BANK], F32, "y")
+                nc.scalar.copy(out=y[:], in_=acc[:])
+                nc.sync.dma_start(out=out_0[rows, xc], in_=y[:])
+            nc.sync.dma_start(out=out2_dst[:, pc], in_=page_codes[:, pc].bitcast(I32))
+        for q in range(4):
+            nc.sync.dma_start(
+                out=out_3[0, 4 * q : 4 * q + 4, :].bitcast(I32),
+                in_=page_plane[32 * q : 32 * q + 4, :].bitcast(I32),
+            )

@@ -49,53 +49,75 @@ def tile_list_broodstock_spawning_board_kernel(
         def bank(index, name):
             return psum.tile([P, BANK], F32, name=name, tag="bank%d" % index)
 
-        scale_rows = keep.tile([P, T], U8, name="scale_rows", align_bytes=64)
-        nc.vector.memset(scale_rows[:].bitcast(I32), 0)
-        nc.gpsimd.dma_start(
-            out=scale_rows[0 : PASSES * 16, :].bitcast(I32),
-            in_=tab_scales.rearrange("a q t -> (a q) t").bitcast(I32),
-        )
+        rows_a = keep.tile([P, T], U8, name="rows_a", align_bytes=64)
+        rows_b = keep.tile([P, T], U8, name="rows_b", align_bytes=64)
         w4_plane = keep.tile([P, PASSES, H], U8, name="w4_plane", align_bytes=64)
-        nc.vector.memset(w4_plane[:].rearrange("p a c -> p (a c)").bitcast(I32), 0)
         v_plane = keep.tile([P, PASSES, S], U8, name="v_plane", align_bytes=64)
+        nc.vector.memset(rows_b[:].bitcast(I32), 0)
+        nc.vector.memset(w4_plane[:].rearrange("p a c -> p (a c)").bitcast(I32), 0)
+        nc.vector.memset(rows_a[32:64, :].bitcast(I32), 0)
+        nc.vector.memset(rows_a[64:128, :].bitcast(I32), 0)
         nc.vector.memset(v_plane[:].rearrange("p a c -> p (a c)").bitcast(I32), 0)
-        for q in range(4):
-            nc.gpsimd.dma_start(
-                out=w4_plane[32 * q : 32 * q + 4, :, :].bitcast(I32),
-                in_=w4_scales[:, 4 * q : 4 * q + 4, :].rearrange("a r c -> r a c").bitcast(I32),
-            )
-
-        gain_col = keep.tile([P, PACK], F32, name="gain_col")
-        nc.gpsimd.dma_start(out=gain_col[:], in_=gain.rearrange("(p t) -> p t", t=PACK))
-        bias_col = keep.tile([P, PACK], F32, name="bias_col")
-        nc.gpsimd.dma_start(out=bias_col[:], in_=bias.rearrange("(p t) -> p t", t=PACK))
         ident = keep.tile([P, P], F32, name="ident")
         make_identity(nc, ident[:])
 
+        scale_src = tab_scales.rearrange("a q t -> (a q) t").bitcast(I32)
         idx = lists.tile([P, S // LANE], U16, name="idx")
         nc.sync.dma_start(idx[:], offs)
-        table = []
+        nc.sync.dma_start(out=rows_a[0:32, :].bitcast(I32), in_=scale_src[0:32, :])
+        table = [keep.tile([P, T], U32, name="table%d" % a, align_bytes=64) for a in range(PASSES)]
         w4_codes = keep.tile([P, PASSES, 2 * H], U8, name="w4_codes", align_bytes=64)
-        for a in range(PASSES):
-            words = keep.tile([P, T], U32, name="table%d" % a, align_bytes=64)
+
+        def load_table(a):
             nc.sync.dma_start(
-                out=words[:].bitcast(I32), in_=tab_words[a].rearrange("p t i -> p (t i)").bitcast(I32)
+                out=table[a][:].bitcast(I32), in_=tab_words[a].rearrange("p t i -> p (t i)").bitcast(I32)
             )
-            table.append(words)
-            if a == 0:
-                nc.sync.dma_start(
-                    out=w4_codes[:].bitcast(I32), in_=w4_words.rearrange("a p c -> p a c").bitcast(I32)
-                )
+
         w1_pieces = [(0, 0, H), (1, 0, H), (2, 0, H // 2), (2, H // 2, H)]
         w1_raw = []
-        for a, c0, c1 in w1_pieces:
+
+        def load_w1(piece):
+            a, c0, c1 = w1_pieces[piece]
             alloc = medium if c1 - c0 == H else small
             raw = alloc([P, PACK, c1 - c0], F32, "w1_raw")
             rows = w1[512 * a : 512 * (a + 1), c0:c1].rearrange("(p j) c -> p j c", j=PACK)
             nc.sync.dma_start(out=raw[:], in_=rows)
             w1_raw.append(raw)
+
+        def place_scales(a, picked_rows, first_row):
+            for q in range(4):
+                r0 = first_row + 4 * q
+                nc.sync.dma_start(
+                    out=v_plane[32 * q : 32 * q + 4, a, :].bitcast(I32),
+                    in_=picked_rows[r0 : r0 + 4, :].bitcast(I32),
+                )
+
+        load_table(0)
+        nc.sync.dma_start(out=rows_b[0:16, :].bitcast(I32), in_=scale_src[32:48, :])
+        nc.sync.dma_start(out=w4_codes[:].bitcast(I32), in_=w4_words.rearrange("a p c -> p a c").bitcast(I32))
+        for q in range(4):
+            nc.sync.dma_start(
+                out=w4_plane[32 * q : 32 * q + 4, :, :].bitcast(I32),
+                in_=w4_scales[:, 4 * q : 4 * q + 4, :].rearrange("a r c -> r a c").bitcast(I32),
+            )
+        load_table(1)
+        picked_a = keep.tile([P, S], U8, name="picked_a", align_bytes=64)
+        nc.vector.tensor_copy(picked_a[:], rows_a[:].indirect(idx[:]))
+        place_scales(0, picked_a, 0)
+        load_table(2)
+        place_scales(1, picked_a, 16)
+        load_w1(0)
+        picked_b = keep.tile([P, S], U8, name="picked_b", align_bytes=64)
+        nc.vector.tensor_copy(picked_b[:], rows_b[:].indirect(idx[:]))
+        place_scales(2, picked_b, 0)
+        for piece in range(1, len(w1_pieces)):
+            load_w1(piece)
         idx2 = lists.tile([P, S // LANE], U16, name="idx2")
         nc.sync.dma_start(idx2[:], offs2)
+        gain_col = keep.tile([P, PACK], F32, name="gain_col")
+        nc.sync.dma_start(out=gain_col[:], in_=gain.rearrange("(p t) -> p t", t=PACK))
+        bias_col = keep.tile([P, PACK], F32, name="bias_col")
+        nc.sync.dma_start(out=bias_col[:], in_=bias.rearrange("(p t) -> p t", t=PACK))
         page, wgs_rows = [], []
         page_src = page0.rearrange("(p t) c -> t p c", t=PACK)
         wgs_src = wgs.rearrange("(s t) j -> t s j", t=PACK)
@@ -110,16 +132,6 @@ def tile_list_broodstock_spawning_board_kernel(
             if t == 0:
                 idx3 = lists.tile([P, M // LANE], U16, name="idx3")
                 nc.sync.dma_start(idx3[:], offs3)
-
-        picked_rows = keep.tile([P, S], U8, name="picked_rows", align_bytes=64)
-        nc.vector.tensor_copy(picked_rows[:], scale_rows[:].indirect(idx[:]))
-        for a in range(PASSES):
-            for q in range(4):
-                r0 = 16 * a + 4 * q
-                nc.gpsimd.dma_start(
-                    out=v_plane[32 * q : 32 * q + 4, a, :].bitcast(I32),
-                    in_=picked_rows[r0 : r0 + 4, :].bitcast(I32),
-                )
 
         v_codes = []
         for a in range(PASSES):
@@ -186,12 +198,14 @@ def tile_list_broodstock_spawning_board_kernel(
                 stop=(piece == len(w1_pieces) - 1),
             )
 
-        for piece in range(2):
-            for j in range(BLOCKS):
-                a_pass(j, piece)
         for j in range(BLOCKS):
-            a_pass(j, 2)
-            a_pass(j, 3)
+            a_pass(j, 0)
+        for piece in (1, 2, 3):
+            for j in range(BLOCKS // 2):
+                a_pass(j, piece)
+        for j in range(BLOCKS // 2, BLOCKS):
+            for piece in (1, 2, 3):
+                a_pass(j, piece)
 
         u_sb = large([P, BLOCKS, H], F32, "u_sb")
         for j in range(BLOCKS):
@@ -205,8 +219,8 @@ def tile_list_broodstock_spawning_board_kernel(
             )
 
         h = [small([P, S], F32, "h") for t in range(PACK)]
-        for half in range(2):
-            for t in range(PACK):
+        for t in range(PACK):
+            for half in range(2):
                 acc = bank(4 * half + t, "h_bank")
                 for jj in range(4):
                     j = 4 * half + jj
@@ -226,76 +240,93 @@ def tile_list_broodstock_spawning_board_kernel(
                     scale=gain_col[:, t : t + 1],
                 )
 
-        w2_raw = medium([P, PACK, N], F32, "w2_raw")
+        w2_raw = keep.tile([P, PACK, N], F32, name="w2_raw")
         nc.sync.dma_start(out=w2_raw[:], in_=w2.rearrange("(p j) n -> p j n", j=PACK))
 
         out1_dst = out_1.rearrange("(p t) c -> t p c", t=PACK)
         page_bf = large([P, PACK, T2], BF16, "page_bf")
-        page_grouped = large([P, T2, PACK], BF16, "page_grouped")
-        x_grouped = medium([P, M, PACK], BF16, "x_grouped")
+        x_grouped = large([P, M, PACK], BF16, "x_grouped")
+        page_grouped = [medium([P, T2 // 2, PACK], BF16, "page_grouped") for half in range(2)]
         w2_grouped = keep.tile([P, N, PACK], BF16, name="w2_grouped", align_bytes=64)
         w2_codes = keep.tile([P, N], U32, name="w2_codes", align_bytes=64)
         w2_plane = keep.tile([P, N], U8, name="w2_plane", align_bytes=64)
 
-        def pieces(count, total):
-            step = total // count
-            return [(i * step, (i + 1) * step) for i in range(count)]
+        def scatter(t, half):
+            c0, c1 = half * BANK, (half + 1) * BANK
+            nc.vector.tensor_tensor(
+                page[t][:].indirect(idx2[:, c0 // LANE : c1 // LANE]),
+                h[t][:, c0:c1],
+                wgs_rows[t][:, c0:c1],
+                MULT,
+            )
+            if half == 1:
+                nc.sync.dma_start(out=out1_dst[t], in_=page[t][:])
 
-        for t in range(PACK):
-            last = t == PACK - 1
-            for c0, c1 in pieces(2 if t == 0 else 1, S):
-                nc.vector.tensor_tensor(
-                    page[t][:].indirect(idx2[:, c0 // LANE : c1 // LANE]),
-                    h[t][:, c0:c1],
-                    wgs_rows[t][:, c0:c1],
-                    MULT,
-                )
-            nc.sync.dma_start(out=out1_dst[t], in_=page[t][:])
-            picked = small([P, M], F32, "picked")
-            for c0, c1 in pieces(2 if last else 1, T2):
-                nc.scalar.copy(out=page_bf[:, t, c0:c1], in_=page[t][:, c0:c1])
-            for c0, c1 in pieces(2 if last else 1, M):
-                nc.vector.tensor_copy(picked[:, c0:c1], page[t][:].indirect(idx3[:, c0 // LANE : c1 // LANE]))
-                nc.scalar.activation(
-                    out=x_grouped[:, c0:c1, t],
-                    in_=picked[:, c0:c1],
-                    func=IDENTITY,
-                    bias=bias_col[:, t : t + 1],
-                )
+        def round_page(t, c0, c1):
+            nc.scalar.copy(out=page_bf[:, t, c0:c1], in_=page[t][:, c0:c1])
+
+        def fetch(t, picked, c0, c1):
+            nc.vector.tensor_copy(picked[:, c0:c1], page[t][:].indirect(idx3[:, c0 // LANE : c1 // LANE]))
+            nc.scalar.activation(
+                out=x_grouped[:, c0:c1, t], in_=picked[:, c0:c1], func=IDENTITY, bias=bias_col[:, t : t + 1]
+            )
+
+        scatter(0, 0)
+        for t in range(PACK - 1):
+            scatter(t, 1)
+            round_page(t, 0, T2)
+            scatter(t + 1, 0)
+            fetch(t, small([P, M], F32, "picked"), 0, M)
             if t == 0:
                 nc.scalar.copy(
                     out=w2_grouped[:].rearrange("p (c i) j -> p c j i", i=4),
                     in_=w2_raw[:].rearrange("p j (c i) -> p c j i", i=4),
                 )
             if t == 1:
-                nc.scalar.copy(out=page_grouped[:, :, 0:2], in_=page_bf[:, 0:2, :].rearrange("p t m -> p m t"))
+                for half in range(2):
+                    nc.scalar.copy(
+                        out=page_grouped[half][:, :, 0:2],
+                        in_=page_bf[:, 0:2, half * 1024 : (half + 1) * 1024].rearrange("p t m -> p m t"),
+                    )
                 for c0, c1 in ((0, 256), (256, N)):
                     nc.vector.quantize_mx(
                         out=w2_codes[:, c0:c1].bitcast(FP8X4),
                         scales=w2_plane[:, c0:c1],
                         in_=w2_grouped[:, c0:c1, :].rearrange("p c j -> p (c j)"),
                     )
+        last = PACK - 1
+        scatter(last, 1)
+        round_page(last, 0, T2 // 2)
+        picked = small([P, M], F32, "picked")
+        fetch(last, picked, 0, BANK)
+        fetch(last, picked, BANK, M)
+        round_page(last, T2 // 2, T2)
 
         page_codes = keep.tile([P, T2], U32, name="page_codes", align_bytes=64)
         page_plane = keep.tile([P, T2], U8, name="page_plane", align_bytes=64)
         x_codes = keep.tile([P, M], U32, name="x_codes", align_bytes=64)
         x_plane = keep.tile([P, M], U8, name="x_plane", align_bytes=64)
         out2_dst = out_2[0].rearrange("p m t -> p (m t)").bitcast(I32)
-        for half in range(2):
-            pc = slice(half * T2 // 2, (half + 1) * T2 // 2)
-            xc = slice(half * BANK, (half + 1) * BANK)
+
+        def page_pair(c0, c1):
             nc.vector.tensor_copy(
-                out=page_grouped[:, pc, 2:4], in_=page_bf[:, 2:4, pc].rearrange("p t m -> p m t")
+                out=page_grouped[c0 // 1024][:, c0 % 1024 : (c1 - 1) % 1024 + 1, 2:4], in_=page_bf[:, 2:4, c0:c1].rearrange("p t m -> p m t")
             )
+
+        def page_quantise(c0, c1):
+            nc.vector.quantize_mx(
+                out=page_codes[:, c0:c1].bitcast(FP8X4),
+                scales=page_plane[:, c0:c1],
+                in_=page_grouped[c0 // 1024][:, c0 % 1024 : (c1 - 1) % 1024 + 1, :].rearrange("p c j -> p (c j)"),
+            )
+            nc.sync.dma_start(out=out2_dst[:, c0:c1], in_=page_codes[:, c0:c1].bitcast(I32))
+
+        def settle(half):
+            xc = slice(half * BANK, (half + 1) * BANK)
             nc.vector.quantize_mx(
                 out=x_codes[:, xc].bitcast(FP8X4),
                 scales=x_plane[:, xc],
                 in_=x_grouped[:, xc, :].rearrange("p c j -> p (c j)"),
-            )
-            nc.vector.quantize_mx(
-                out=page_codes[:, pc].bitcast(FP8X4),
-                scales=page_plane[:, pc],
-                in_=page_grouped[:, pc, :].rearrange("p c j -> p (c j)"),
             )
             for n in range(N // P):
                 rows = slice(n * P, (n + 1) * P)
@@ -312,7 +343,15 @@ def tile_list_broodstock_spawning_board_kernel(
                 y = small([P, BANK], F32, "y")
                 nc.scalar.copy(out=y[:], in_=acc[:])
                 nc.sync.dma_start(out=out_0[rows, xc], in_=y[:])
-            nc.sync.dma_start(out=out2_dst[:, pc], in_=page_codes[:, pc].bitcast(I32))
+
+        page_pair(0, 1024)
+        settle(0)
+        page_quantise(0, 1024)
+        settle(1)
+        page_pair(1024, 1536)
+        page_pair(1536, 2048)
+        page_quantise(1024, 1536)
+        page_quantise(1536, 2048)
         for q in range(4):
             nc.sync.dma_start(
                 out=out_3[0, 4 * q : 4 * q + 4, :].bitcast(I32),

@@ -44,7 +44,7 @@ def tile_list_broodstock_spawning_board_kernel(
             return share.tile(shape, dtype, name=name, tag="medium", bufs=2, align_bytes=64)
 
         def large(shape, dtype, name):
-            return share.tile(shape, dtype, name=name, tag="large", bufs=2, align_bytes=64)
+            return share.tile(shape, dtype, name=name, tag="large", bufs=4, align_bytes=64)
 
         def bank(index, name):
             return psum.tile([P, BANK], F32, name=name, tag="bank%d" % index)
@@ -70,7 +70,8 @@ def tile_list_broodstock_spawning_board_kernel(
 
         def load_table(a):
             nc.sync.dma_start(
-                out=table[a][:].bitcast(I32), in_=tab_words[a].rearrange("p t i -> p (t i)").bitcast(I32)
+                out=table[a][:].bitcast(I32),
+                in_=tab_words[a].rearrange("p t i -> p (t i)").bitcast(I32),
             )
 
         w1_pieces = [(0, 0, H), (1, 0, H), (2, 0, H // 2), (2, H // 2, H)]
@@ -85,20 +86,19 @@ def tile_list_broodstock_spawning_board_kernel(
             w1_raw.append(raw)
 
         def place_scales(a, picked_rows, first_row):
-            for q in range(4):
-                r0 = first_row + 4 * q
+            for r in range(4):
                 nc.sync.dma_start(
-                    out=v_plane[32 * q : 32 * q + 4, a, :].bitcast(I32),
-                    in_=picked_rows[r0 : r0 + 4, :].bitcast(I32),
+                    out=v_plane[r:P:32, a, :].bitcast(I32),
+                    in_=picked_rows[first_row + r : first_row + 16 : 4, :].bitcast(I32),
                 )
 
         load_table(0)
         nc.sync.dma_start(out=rows_b[0:16, :].bitcast(I32), in_=scale_src[32:48, :])
         nc.sync.dma_start(out=w4_codes[:].bitcast(I32), in_=w4_words.rearrange("a p c -> p a c").bitcast(I32))
-        for q in range(4):
+        for r in range(4):
             nc.sync.dma_start(
-                out=w4_plane[32 * q : 32 * q + 4, :, :].bitcast(I32),
-                in_=w4_scales[:, 4 * q : 4 * q + 4, :].rearrange("a r c -> r a c").bitcast(I32),
+                out=w4_plane[r:P:32, :, :].bitcast(I32),
+                in_=w4_scales.rearrange("a (q r) c -> r q a c", r=4)[r].bitcast(I32),
             )
         load_table(1)
         picked_a = keep.tile([P, S], U8, name="picked_a", align_bytes=64)
@@ -116,8 +116,6 @@ def tile_list_broodstock_spawning_board_kernel(
         nc.sync.dma_start(idx2[:], offs2)
         gain_col = keep.tile([P, PACK], F32, name="gain_col")
         nc.sync.dma_start(out=gain_col[:], in_=gain.rearrange("(p t) -> p t", t=PACK))
-        bias_col = keep.tile([P, PACK], F32, name="bias_col")
-        nc.sync.dma_start(out=bias_col[:], in_=bias.rearrange("(p t) -> p t", t=PACK))
         page, wgs_rows = [], []
         page_src = page0.rearrange("(p t) c -> t p c", t=PACK)
         wgs_src = wgs.rearrange("(s t) j -> t s j", t=PACK)
@@ -126,12 +124,15 @@ def tile_list_broodstock_spawning_board_kernel(
             nc.sync.dma_start(out=board[:], in_=page_src[t])
             page.append(board)
             factor = keep.tile([P, S], F32, name="wgs%d" % t, align_bytes=64)
-            for q in (0, 2, 1, 3):
-                nc.sync.dma_start(out=factor[32 * q : 32 * (q + 1), :], in_=wgs_src[t])
+            for c0, c1 in ((0, BANK), (BANK, S)) if t == 0 else ((0, S),):
+                for q in (0, 2, 1, 3):
+                    nc.sync.dma_start(out=factor[32 * q : 32 * (q + 1), c0:c1], in_=wgs_src[t][:, c0:c1])
             wgs_rows.append(factor)
             if t == 0:
                 idx3 = lists.tile([P, M // LANE], U16, name="idx3")
                 nc.sync.dma_start(idx3[:], offs3)
+                bias_col = keep.tile([P, PACK], F32, name="bias_col")
+                nc.sync.dma_start(out=bias_col[:], in_=bias.rearrange("(p t) -> p t", t=PACK))
 
         v_codes = []
         for a in range(PASSES):
@@ -159,10 +160,10 @@ def tile_list_broodstock_spawning_board_kernel(
                     start=(a == 0),
                     stop=(a == PASSES - 1),
                 )
-        b_sb = large([P, BLOCKS, H], F32, "b_sb")
+        b_sb = [large([P, BLOCKS // 2, H], F32, "b_sb") for half in range(2)]
         for j in range(BLOCKS):
             nc.scalar.activation(
-                out=b_sb[:, j, :].rearrange("p (t m) -> p t m", t=PACK),
+                out=b_sb[j // 4][:, j % 4, :].rearrange("p (t m) -> p t m", t=PACK),
                 in_=b_banks[j][:].rearrange("p (m t) -> p t m", t=PACK),
                 func=IDENTITY,
             )
@@ -207,11 +208,11 @@ def tile_list_broodstock_spawning_board_kernel(
             for piece in (1, 2, 3):
                 a_pass(j, piece)
 
-        u_sb = large([P, BLOCKS, H], F32, "u_sb")
+        u_sb = [large([P, BLOCKS // 2, H], F32, "u_sb") for half in range(2)]
         for j in range(BLOCKS):
             nc.vector.scalar_tensor_tensor(
-                out=u_sb[:, j, :].rearrange("p (t m) -> p t m", t=PACK),
-                in0=b_sb[:, j, :].rearrange("p (t m) -> p t m", t=PACK),
+                out=u_sb[j // 4][:, j % 4, :].rearrange("p (t m) -> p t m", t=PACK),
+                in0=b_sb[j // 4][:, j % 4, :].rearrange("p (t m) -> p t m", t=PACK),
                 scalar=1.0,
                 in1=a_banks[j][:].rearrange("p (m t) -> p t m", t=PACK),
                 op0=ADD,
@@ -223,11 +224,10 @@ def tile_list_broodstock_spawning_board_kernel(
             for half in range(2):
                 acc = bank(4 * half + t, "h_bank")
                 for jj in range(4):
-                    j = 4 * half + jj
                     for first, src in ((True, u_sb), (False, b_sb)):
                         nc.tensor.matmul(
                             acc[:, jj * P : (jj + 1) * P],
-                            src[:, j, t * P : (t + 1) * P],
+                            src[half][:, jj, t * P : (t + 1) * P],
                             ident[:],
                             start=first,
                             stop=not first,
@@ -240,13 +240,12 @@ def tile_list_broodstock_spawning_board_kernel(
                     scale=gain_col[:, t : t + 1],
                 )
 
-        w2_raw = keep.tile([P, PACK, N], F32, name="w2_raw")
+        w2_raw = medium([P, PACK, N], F32, "w2_raw")
         nc.sync.dma_start(out=w2_raw[:], in_=w2.rearrange("(p j) n -> p j n", j=PACK))
 
         out1_dst = out_1.rearrange("(p t) c -> t p c", t=PACK)
-        page_bf = large([P, PACK, T2], BF16, "page_bf")
-        x_grouped = large([P, M, PACK], BF16, "x_grouped")
-        page_grouped = [medium([P, T2 // 2, PACK], BF16, "page_grouped") for half in range(2)]
+        x_pairs = [large([P, 2, M // 2, 2], BF16, "x_pairs") for half in range(2)]
+        page_pairs = [large([P, 2, T2 // 2, 2], BF16, "page_pairs") for half in range(2)]
         w2_grouped = keep.tile([P, N, PACK], BF16, name="w2_grouped", align_bytes=64)
         w2_codes = keep.tile([P, N], U32, name="w2_codes", align_bytes=64)
         w2_plane = keep.tile([P, N], U8, name="w2_plane", align_bytes=64)
@@ -263,31 +262,36 @@ def tile_list_broodstock_spawning_board_kernel(
                 nc.sync.dma_start(out=out1_dst[t], in_=page[t][:])
 
         def round_page(t, c0, c1):
-            nc.scalar.copy(out=page_bf[:, t, c0:c1], in_=page[t][:, c0:c1])
+            half, first = c0 // (T2 // 2), c0 % (T2 // 2)
+            nc.scalar.copy(out=page_pairs[half][:, t // 2, first : first + c1 - c0, t % 2], in_=page[t][:, c0:c1])
 
         def fetch(t, picked, c0, c1):
             nc.vector.tensor_copy(picked[:, c0:c1], page[t][:].indirect(idx3[:, c0 // LANE : c1 // LANE]))
+
+        def add_bias(t, picked, half):
             nc.scalar.activation(
-                out=x_grouped[:, c0:c1, t], in_=picked[:, c0:c1], func=IDENTITY, bias=bias_col[:, t : t + 1]
+                out=x_pairs[half][:, t // 2, :, t % 2],
+                in_=picked[:, half * BANK : (half + 1) * BANK],
+                func=IDENTITY,
+                bias=bias_col[:, t : t + 1],
             )
 
         scatter(0, 0)
         for t in range(PACK - 1):
             scatter(t, 1)
-            round_page(t, 0, T2)
+            for half in range(2):
+                round_page(t, half * 1024, (half + 1) * 1024)
             scatter(t + 1, 0)
-            fetch(t, small([P, M], F32, "picked"), 0, M)
-            if t == 0:
+            picked = small([P, M], F32, "picked")
+            fetch(t, picked, 0, M)
+            for half in range(2):
+                add_bias(t, picked, half)
+            if t == 1:
                 nc.scalar.copy(
                     out=w2_grouped[:].rearrange("p (c i) j -> p c j i", i=4),
                     in_=w2_raw[:].rearrange("p j (c i) -> p c j i", i=4),
                 )
-            if t == 1:
-                for half in range(2):
-                    nc.scalar.copy(
-                        out=page_grouped[half][:, :, 0:2],
-                        in_=page_bf[:, 0:2, half * 1024 : (half + 1) * 1024].rearrange("p t m -> p m t"),
-                    )
+            if t == 2:
                 for c0, c1 in ((0, 256), (256, N)):
                     nc.vector.quantize_mx(
                         out=w2_codes[:, c0:c1].bitcast(FP8X4),
@@ -296,11 +300,12 @@ def tile_list_broodstock_spawning_board_kernel(
                     )
         last = PACK - 1
         scatter(last, 1)
-        round_page(last, 0, T2 // 2)
         picked = small([P, M], F32, "picked")
-        fetch(last, picked, 0, BANK)
-        fetch(last, picked, BANK, M)
-        round_page(last, T2 // 2, T2)
+        for half in range(2):
+            fetch(last, picked, half * BANK, (half + 1) * BANK)
+            add_bias(last, picked, half)
+        for quarter in range(4):
+            round_page(last, quarter * 512, (quarter + 1) * 512)
 
         page_codes = keep.tile([P, T2], U32, name="page_codes", align_bytes=64)
         page_plane = keep.tile([P, T2], U8, name="page_plane", align_bytes=64)
@@ -308,25 +313,31 @@ def tile_list_broodstock_spawning_board_kernel(
         x_plane = keep.tile([P, M], U8, name="x_plane", align_bytes=64)
         out2_dst = out_2[0].rearrange("p m t -> p (m t)").bitcast(I32)
 
-        def page_pair(c0, c1):
-            nc.vector.tensor_copy(
-                out=page_grouped[c0 // 1024][:, c0 % 1024 : (c1 - 1) % 1024 + 1, 2:4], in_=page_bf[:, 2:4, c0:c1].rearrange("p t m -> p m t")
-            )
+        def weave(pairs, c0, c1, grouped):
+            words = pairs[:].rearrange("p u m e -> p u (m e)").bitcast(I32)
+            nc.vector.tensor_copy(out=grouped[:].bitcast(I32), in_=words[:, :, c0:c1].rearrange("p u m -> p m u"))
 
-        def page_quantise(c0, c1):
+        def page_quantise(grouped, c0, c1):
             nc.vector.quantize_mx(
                 out=page_codes[:, c0:c1].bitcast(FP8X4),
                 scales=page_plane[:, c0:c1],
-                in_=page_grouped[c0 // 1024][:, c0 % 1024 : (c1 - 1) % 1024 + 1, :].rearrange("p c j -> p (c j)"),
+                in_=grouped[:].rearrange("p c j -> p (c j)"),
             )
             nc.sync.dma_start(out=out2_dst[:, c0:c1], in_=page_codes[:, c0:c1].bitcast(I32))
 
-        def settle(half):
+        def store_scales(c0, c1):
+            for r in range(4):
+                nc.sync.dma_start(
+                    out=out_3[0].rearrange("(q r) m -> r q m", r=4)[r][:, c0:c1].bitcast(I32),
+                    in_=page_plane[r:P:32, c0:c1].bitcast(I32),
+                )
+
+        def settle(half, grouped):
             xc = slice(half * BANK, (half + 1) * BANK)
             nc.vector.quantize_mx(
                 out=x_codes[:, xc].bitcast(FP8X4),
                 scales=x_plane[:, xc],
-                in_=x_grouped[:, xc, :].rearrange("p c j -> p (c j)"),
+                in_=grouped[:].rearrange("p c j -> p (c j)"),
             )
             for n in range(N // P):
                 rows = slice(n * P, (n + 1) * P)
@@ -344,16 +355,18 @@ def tile_list_broodstock_spawning_board_kernel(
                 nc.scalar.copy(out=y[:], in_=acc[:])
                 nc.sync.dma_start(out=out_0[rows, xc], in_=y[:])
 
-        page_pair(0, 1024)
-        settle(0)
-        page_quantise(0, 1024)
-        settle(1)
-        page_pair(1024, 1536)
-        page_pair(1536, 2048)
-        page_quantise(1024, 1536)
-        page_quantise(1536, 2048)
-        for q in range(4):
-            nc.sync.dma_start(
-                out=out_3[0, 4 * q : 4 * q + 4, :].bitcast(I32),
-                in_=page_plane[32 * q : 32 * q + 4, :].bitcast(I32),
-            )
+        x_grouped = [small([P, BANK, PACK], BF16, "x_grouped") for half in range(2)]
+        weave(x_pairs[0], 0, BANK, x_grouped[0])
+        weave(x_pairs[1], 0, BANK, x_grouped[1])
+        settle(0, x_grouped[0])
+        first = large([P, T2 // 2, PACK], BF16, "page_grouped")
+        weave(page_pairs[0], 0, T2 // 2, first)
+        settle(1, x_grouped[1])
+        page_quantise(first, 0, 1024)
+        store_scales(0, 1024)
+        rest = [medium([P, T2 // 4, PACK], BF16, "page_grouped") for part in range(2)]
+        for part in range(2):
+            weave(page_pairs[1], part * 512, (part + 1) * 512, rest[part])
+        for part in range(2):
+            page_quantise(rest[part], 1024 + part * 512, 1024 + (part + 1) * 512)
+        store_scales(1024, 2048)

@@ -85,8 +85,8 @@ def tile_list_broodstock_spawning_board_kernel(
             nc.sync.dma_start(out=raw[:], in_=rows)
             w1_raw.append(raw)
 
-        def place_scales(a, picked_rows, first_row):
-            for r in range(4):
+        def place_scales(a, picked_rows, first_row, lanes):
+            for r in lanes:
                 nc.sync.dma_start(
                     out=v_plane[r:P:32, a, :].bitcast(I32),
                     in_=picked_rows[first_row + r : first_row + 16 : 4, :].bitcast(I32),
@@ -103,14 +103,14 @@ def tile_list_broodstock_spawning_board_kernel(
         load_table(1)
         picked_a = keep.tile([P, S], U8, name="picked_a", align_bytes=64)
         nc.vector.tensor_copy(picked_a[:], rows_a[:].indirect(idx[:]))
-        place_scales(0, picked_a, 0)
+        place_scales(0, picked_a, 0, range(4))
+        place_scales(1, picked_a, 16, range(2))
         load_table(2)
-        place_scales(1, picked_a, 16)
-        load_w1(0)
+        place_scales(1, picked_a, 16, range(2, 4))
         picked_b = keep.tile([P, S], U8, name="picked_b", align_bytes=64)
         nc.vector.tensor_copy(picked_b[:], rows_b[:].indirect(idx[:]))
-        place_scales(2, picked_b, 0)
-        for piece in range(1, len(w1_pieces)):
+        place_scales(2, picked_b, 0, range(4))
+        for piece in range(len(w1_pieces)):
             load_w1(piece)
         idx2 = lists.tile([P, S // LANE], U16, name="idx2")
         nc.sync.dma_start(idx2[:], offs2)
@@ -172,7 +172,8 @@ def tile_list_broodstock_spawning_board_kernel(
         for (a, c0, c1), raw in zip(w1_pieces, w1_raw):
             width = c1 - c0
             grouped = small([P, width, PACK], BF16, "w1_grouped")
-            nc.vector.tensor_copy(
+            regroup = nc.scalar.copy if (a, c0) == (PASSES - 1, 0) else nc.vector.tensor_copy
+            regroup(
                 out=grouped[:].rearrange("p (c i) j -> p c j i", i=4),
                 in_=raw[:].rearrange("p j (c i) -> p c j i", i=4),
             )
@@ -250,15 +251,14 @@ def tile_list_broodstock_spawning_board_kernel(
         w2_codes = keep.tile([P, N], U32, name="w2_codes", align_bytes=64)
         w2_plane = keep.tile([P, N], U8, name="w2_plane", align_bytes=64)
 
-        def scatter(t, half):
-            c0, c1 = half * BANK, (half + 1) * BANK
+        def scatter(t, c0, c1):
             nc.vector.tensor_tensor(
                 page[t][:].indirect(idx2[:, c0 // LANE : c1 // LANE]),
                 h[t][:, c0:c1],
                 wgs_rows[t][:, c0:c1],
                 MULT,
             )
-            if half == 1:
+            if c1 == S:
                 nc.sync.dma_start(out=out1_dst[t], in_=page[t][:])
 
         def round_page(t, c0, c1):
@@ -276,12 +276,12 @@ def tile_list_broodstock_spawning_board_kernel(
                 bias=bias_col[:, t : t + 1],
             )
 
-        scatter(0, 0)
+        scatter(0, 0, BANK)
+        scatter(0, BANK, S)
         for t in range(PACK - 1):
-            scatter(t, 1)
             for half in range(2):
                 round_page(t, half * 1024, (half + 1) * 1024)
-            scatter(t + 1, 0)
+            scatter(t + 1, 0, S if t + 1 < PACK - 1 else BANK)
             picked = small([P, M], F32, "picked")
             fetch(t, picked, 0, M)
             for half in range(2):
@@ -299,7 +299,7 @@ def tile_list_broodstock_spawning_board_kernel(
                         in_=w2_grouped[:, c0:c1, :].rearrange("p c j -> p (c j)"),
                     )
         last = PACK - 1
-        scatter(last, 1)
+        scatter(last, BANK, S)
         picked = small([P, M], F32, "picked")
         for half in range(2):
             fetch(last, picked, half * BANK, (half + 1) * BANK)
@@ -363,10 +363,9 @@ def tile_list_broodstock_spawning_board_kernel(
         weave(page_pairs[0], 0, T2 // 2, first)
         settle(1, x_grouped[1])
         page_quantise(first, 0, 1024)
-        store_scales(0, 1024)
         rest = [medium([P, T2 // 4, PACK], BF16, "page_grouped") for part in range(2)]
         for part in range(2):
             weave(page_pairs[1], part * 512, (part + 1) * 512, rest[part])
         for part in range(2):
             page_quantise(rest[part], 1024 + part * 512, 1024 + (part + 1) * 512)
-        store_scales(1024, 2048)
+        store_scales(0, T2)

from contextlib import ExitStack

import concourse.mybir as mybir
from concourse.masks import make_identity

K, H, N, T, S, T2, M = 1536, 512, 384, 4096, 1024, 2048, 1024
FLOPS = 2 * (2 * K * H * S + H * N * M)

F32 = mybir.dt.float32
BF16 = mybir.dt.bfloat16
I32 = mybir.dt.int32
U32 = mybir.dt.uint32
U16 = mybir.dt.uint16
U8 = mybir.dt.uint8
FP8X4 = mybir.dt.float8_e4m3fn_x4
FP4X4 = mybir.dt.float4_e2m1fn_x4
ADD = mybir.AluOpType.add
MULT = mybir.AluOpType.mult
IDENTITY = mybir.ActivationFunctionType.Identity

P = 128
PACK = 4
PASSES = K // (P * PACK)
BANK = 512
BLOCKS = S // P
LANE = 16


def tile_list_broodstock_spawning_board_kernel(
    tc, tab_words, tab_scales, offs, w1, w4_words, w4_scales, gain, wgs, page0, offs2, offs3, bias, w2,
    out_0, out_1, out_2, out_3,
):
    nc = tc.nc
    with ExitStack() as ctx:
        lists = ctx.enter_context(tc.tile_pool(name="lists", bufs=1))
        keep = ctx.enter_context(tc.tile_pool(name="keep", bufs=1))
        share = ctx.enter_context(tc.tile_pool(name="share", bufs=1))
        psum = ctx.enter_context(tc.psum_pool(name="psum", bufs=1))

        def small(shape, dtype, name):
            return share.tile(shape, dtype, name=name, tag="small", bufs=6, align_bytes=64)

        def medium(shape, dtype, name):
            return share.tile(shape, dtype, name=name, tag="medium", bufs=2, align_bytes=64)

        def large(shape, dtype, name):
            return share.tile(shape, dtype, name=name, tag="large", bufs=4, align_bytes=64)

        def bank(index, name):
            return psum.tile([P, BANK], F32, name=name, tag="bank%d" % index)

        rows_a = keep.tile([P, T], U8, name="rows_a", align_bytes=64)
        rows_b = keep.tile([P, T], U8, name="rows_b", align_bytes=64)
        w4_plane = keep.tile([P, PASSES, H], U8, name="w4_plane", align_bytes=64)
        v_plane = keep.tile([P, PASSES, S], U8, name="v_plane", align_bytes=64)
        nc.vector.memset(rows_b[:].bitcast(I32), 0)
        nc.vector.memset(w4_plane[:].rearrange("p a c -> p (a c)").bitcast(I32), 0)
        nc.vector.memset(rows_a[32:64, :].bitcast(I32), 0)
        nc.vector.memset(rows_a[64:128, :].bitcast(I32), 0)
        nc.vector.memset(v_plane[:].rearrange("p a c -> p (a c)").bitcast(I32), 0)
        ident = keep.tile([P, P], F32, name="ident")
        make_identity(nc, ident[:])

        scale_src = tab_scales.rearrange("a q t -> (a q) t").bitcast(I32)
        idx = lists.tile([P, S // LANE], U16, name="idx")
        nc.sync.dma_start(idx[:], offs)
        nc.sync.dma_start(out=rows_a[0:32, :].bitcast(I32), in_=scale_src[0:32, :])
        table = [keep.tile([P, T], U32, name="table%d" % a, align_bytes=64) for a in range(PASSES)]
        w4_codes = keep.tile([P, PASSES, 2 * H], U8, name="w4_codes", align_bytes=64)

        def load_table(a):
            nc.sync.dma_start(
                out=table[a][:].bitcast(I32),
                in_=tab_words[a].rearrange("p t i -> p (t i)").bitcast(I32),
            )

        w1_pieces = [(0, 0, H), (1, 0, H), (2, 0, H // 2), (2, H // 2, H)]
        w1_raw = []

        def load_w1(piece):
            a, c0, c1 = w1_pieces[piece]
            alloc = medium if c1 - c0 == H else small
            raw = alloc([P, PACK, c1 - c0], F32, "w1_raw")
            rows = w1[512 * a : 512 * (a + 1), c0:c1].rearrange("(p j) c -> p j c", j=PACK)
            nc.sync.dma_start(out=raw[:], in_=rows)
            w1_raw.append(raw)

        def place_scales(a, picked_rows, first_row, lanes):
            for r in lanes:
                nc.sync.dma_start(
                    out=v_plane[r:P:32, a, :].bitcast(I32),
                    in_=picked_rows[first_row + r : first_row + 16 : 4, :].bitcast(I32),
                )

        load_table(0)
        nc.sync.dma_start(out=rows_b[0:16, :].bitcast(I32), in_=scale_src[32:48, :])
        nc.sync.dma_start(out=w4_codes[:].bitcast(I32), in_=w4_words.rearrange("a p c -> p a c").bitcast(I32))
        for r in range(4):
            nc.sync.dma_start(
                out=w4_plane[r:P:32, :, :].bitcast(I32),
                in_=w4_scales.rearrange("a (q r) c -> r q a c", r=4)[r].bitcast(I32),
            )
        load_table(1)
        picked_a = keep.tile([P, S], U8, name="picked_a", align_bytes=64)
        nc.vector.tensor_copy(picked_a[:], rows_a[:].indirect(idx[:]))
        place_scales(0, picked_a, 0, range(4))
        place_scales(1, picked_a, 16, range(2))
        load_table(2)
        place_scales(1, picked_a, 16, range(2, 4))
        picked_b = keep.tile([P, S], U8, name="picked_b", align_bytes=64)
        nc.vector.tensor_copy(picked_b[:], rows_b[:].indirect(idx[:]))
        place_scales(2, picked_b, 0, range(4))
        for piece in range(len(w1_pieces)):
            load_w1(piece)
        idx2 = lists.tile([P, S // LANE], U16, name="idx2")
        nc.sync.dma_start(idx2[:], offs2)
        gain_col = keep.tile([P, PACK], F32, name="gain_col")
        nc.sync.dma_start(out=gain_col[:], in_=gain.rearrange("(p t) -> p t", t=PACK))
        page, wgs_rows = [], []
        page_src = page0.rearrange("(p t) c -> t p c", t=PACK)
        wgs_src = wgs.rearrange("(s t) j -> t s j", t=PACK)
        for t in range(PACK):
            board = keep.tile([P, T2], F32, name="page%d" % t, align_bytes=64)
            nc.sync.dma_start(out=board[:], in_=page_src[t])
            page.append(board)
            factor = keep.tile([P, S], F32, name="wgs%d" % t, align_bytes=64)
            for c0, c1 in ((0, BANK), (BANK, S)) if t == 0 else ((0, S),):
                for q in (0, 2, 1, 3):
                    nc.sync.dma_start(out=factor[32 * q : 32 * (q + 1), c0:c1], in_=wgs_src[t][:, c0:c1])
            wgs_rows.append(factor)
            if t == 0:
                idx3 = lists.tile([P, M // LANE], U16, name="idx3")
                nc.sync.dma_start(idx3[:], offs3)
                bias_col = keep.tile([P, PACK], F32, name="bias_col")
                nc.sync.dma_start(out=bias_col[:], in_=bias.rearrange("(p t) -> p t", t=PACK))

        v_codes = []
        for a in range(PASSES):
            picked = keep.tile([P, S], U32, name="v_codes%d" % a, align_bytes=64)
            if a < PASSES - 1:
                nc.vector.tensor_copy(picked[:], table[a][:].indirect(idx[:]))
            else:
                for half in range(2):
                    nc.vector.tensor_copy(
                        picked[:, half * BANK : (half + 1) * BANK],
                        table[a][:].indirect(idx[:, half * 32 : (half + 1) * 32]),
                    )
            v_codes.append(picked)

        b_banks = [bank(j, "b_bank") for j in range(BLOCKS)]
        for a in range(PASSES):
            for j in range(BLOCKS):
                cols = slice(j * P, (j + 1) * P)
                nc.tensor.matmul_mx(
                    out=b_banks[j][:],
                    lhsT=v_codes[a][:, cols].bitcast(FP8X4),
                    lhsT_scale=v_plane[:, a, cols],
                    rhs=w4_codes[:, a, :].bitcast(FP4X4),
                    rhs_scale=w4_plane[:, a, :],
                    start=(a == 0),
                    stop=(a == PASSES - 1),
                )
        b_sb = [large([P, BLOCKS // 2, H], F32, "b_sb") for half in range(2)]
        for j in range(BLOCKS):
            nc.scalar.activation(
                out=b_sb[j // 4][:, j % 4, :].rearrange("p (t m) -> p t m", t=PACK),
                in_=b_banks[j][:].rearrange("p (m t) -> p t m", t=PACK),
                func=IDENTITY,
            )

        w1_codes, w1_plane = [], []
        for (a, c0, c1), raw in zip(w1_pieces, w1_raw):
            width = c1 - c0
            grouped = small([P, width, PACK], BF16, "w1_grouped")
            regroup = nc.scalar.copy if (a, c0) == (PASSES - 1, 0) else nc.vector.tensor_copy
            regroup(
                out=grouped[:].rearrange("p (c i) j -> p c j i", i=4),
                in_=raw[:].rearrange("p j (c i) -> p c j i", i=4),
            )
            codes = keep.tile([P, width], U32, name="w1_codes%d_%d" % (a, c0), align_bytes=64)
            plane = keep.tile([P, width], U8, name="w1_plane%d_%d" % (a, c0), align_bytes=64)
            nc.vector.quantize_mx(
                out=codes[:].bitcast(FP8X4), scales=plane[:], in_=grouped[:].rearrange("p c j -> p (c j)")
            )
            w1_codes.append(codes)
            w1_plane.append(plane)

        a_banks = [bank(j, "a_bank") for j in range(BLOCKS)]

        def a_pass(j, piece):
            a, c0, c1 = w1_pieces[piece]
            cols = slice(j * P, (j + 1) * P)
            nc.tensor.matmul_mx(
                out=a_banks[j][:, c0:c1],
                lhsT=v_codes[a][:, cols].bitcast(FP8X4),
                lhsT_scale=v_plane[:, a, cols],
                rhs=w1_codes[piece][:].bitcast(FP8X4),
                rhs_scale=w1_plane[piece][:],
                start=(piece == 0),
                stop=(piece == len(w1_pieces) - 1),
            )

        for j in range(BLOCKS):
            a_pass(j, 0)
        for piece in (1, 2, 3):
            for j in range(BLOCKS // 2):
                a_pass(j, piece)
        for j in range(BLOCKS // 2, BLOCKS):
            for piece in (1, 2, 3):
                a_pass(j, piece)

        u_sb = [large([P, BLOCKS // 2, H], F32, "u_sb") for half in range(2)]
        for j in range(BLOCKS):
            nc.vector.scalar_tensor_tensor(
                out=u_sb[j // 4][:, j % 4, :].rearrange("p (t m) -> p t m", t=PACK),
                in0=b_sb[j // 4][:, j % 4, :].rearrange("p (t m) -> p t m", t=PACK),
                scalar=1.0,
                in1=a_banks[j][:].rearrange("p (m t) -> p t m", t=PACK),
                op0=ADD,
                op1=MULT,
            )

        h = [small([P, S], F32, "h") for t in range(PACK)]
        for t in range(PACK):
            for half in range(2):
                acc = bank(4 * half + t, "h_bank")
                for jj in range(4):
                    for first, src in ((True, u_sb), (False, b_sb)):
                        nc.tensor.matmul(
                            acc[:, jj * P : (jj + 1) * P],
                            src[half][:, jj, t * P : (t + 1) * P],
                            ident[:],
                            start=first,
                            stop=not first,
                            is_transpose=True,
                        )
                nc.scalar.activation(
                    out=h[t][:, half * BANK : (half + 1) * BANK],
                    in_=acc[:],
                    func=IDENTITY,
                    scale=gain_col[:, t : t + 1],
                )

        w2_raw = medium([P, PACK, N], F32, "w2_raw")
        nc.sync.dma_start(out=w2_raw[:], in_=w2.rearrange("(p j) n -> p j n", j=PACK))

        out1_dst = out_1.rearrange("(p t) c -> t p c", t=PACK)
        x_pairs = [large([P, 2, M // 2, 2], BF16, "x_pairs") for half in range(2)]
        page_pairs = [large([P, 2, T2 // 2, 2], BF16, "page_pairs") for half in range(2)]
        w2_grouped = keep.tile([P, N, PACK], BF16, name="w2_grouped", align_bytes=64)
        w2_codes = keep.tile([P, N], U32, name="w2_codes", align_bytes=64)
        w2_plane = keep.tile([P, N], U8, name="w2_plane", align_bytes=64)

        def scatter(t, c0, c1):
            nc.vector.tensor_tensor(
                page[t][:].indirect(idx2[:, c0 // LANE : c1 // LANE]),
                h[t][:, c0:c1],
                wgs_rows[t][:, c0:c1],
                MULT,
            )
            if c1 == S:
                nc.sync.dma_start(out=out1_dst[t], in_=page[t][:])

        def round_page(t, c0, c1):
            half, first = c0 // (T2 // 2), c0 % (T2 // 2)
            nc.scalar.copy(out=page_pairs[half][:, t // 2, first : first + c1 - c0, t % 2], in_=page[t][:, c0:c1])

        def fetch(t, picked, c0, c1):
            nc.vector.tensor_copy(picked[:, c0:c1], page[t][:].indirect(idx3[:, c0 // LANE : c1 // LANE]))

        def add_bias(t, picked, half):
            nc.scalar.activation(
                out=x_pairs[half][:, t // 2, :, t % 2],
                in_=picked[:, half * BANK : (half + 1) * BANK],
                func=IDENTITY,
                bias=bias_col[:, t : t + 1],
            )

        scatter(0, 0, BANK)
        scatter(0, BANK, S)
        for t in range(PACK - 1):
            for half in range(2):
                round_page(t, half * 1024, (half + 1) * 1024)
            scatter(t + 1, 0, S if t + 1 < PACK - 1 else BANK)
            picked = small([P, M], F32, "picked")
            fetch(t, picked, 0, M)
            for half in range(2):
                add_bias(t, picked, half)
            if t == 1:
                nc.scalar.copy(
                    out=w2_grouped[:].rearrange("p (c i) j -> p c j i", i=4),
                    in_=w2_raw[:].rearrange("p j (c i) -> p c j i", i=4),
                )
            if t == 2:
                for c0, c1 in ((0, 256), (256, N)):
                    nc.vector.quantize_mx(
                        out=w2_codes[:, c0:c1].bitcast(FP8X4),
                        scales=w2_plane[:, c0:c1],
                        in_=w2_grouped[:, c0:c1, :].rearrange("p c j -> p (c j)"),
                    )
        last = PACK - 1
        scatter(last, BANK, S)
        picked = small([P, M], F32, "picked")
        for half in range(2):
            fetch(last, picked, half * BANK, (half + 1) * BANK)
            add_bias(last, picked, half)
        for quarter in range(4):
            round_page(last, quarter * 512, (quarter + 1) * 512)

        page_codes = keep.tile([P, T2], U32, name="page_codes", align_bytes=64)
        page_plane = keep.tile([P, T2], U8, name="page_plane", align_bytes=64)
        x_codes = keep.tile([P, M], U32, name="x_codes", align_bytes=64)
        x_plane = keep.tile([P, M], U8, name="x_plane", align_bytes=64)
        out2_dst = out_2[0].rearrange("p m t -> p (m t)").bitcast(I32)

        def weave(pairs, c0, c1, grouped):
            words = pairs[:].rearrange("p u m e -> p u (m e)").bitcast(I32)
            nc.vector.tensor_copy(out=grouped[:].bitcast(I32), in_=words[:, :, c0:c1].rearrange("p u m -> p m u"))

        def page_quantise(grouped, c0, c1):
            nc.vector.quantize_mx(
                out=page_codes[:, c0:c1].bitcast(FP8X4),
                scales=page_plane[:, c0:c1],
                in_=grouped[:].rearrange("p c j -> p (c j)"),
            )
            nc.sync.dma_start(out=out2_dst[:, c0:c1], in_=page_codes[:, c0:c1].bitcast(I32))

        def store_scales(c0, c1):
            for r in range(4):
                nc.sync.dma_start(
                    out=out_3[0].rearrange("(q r) m -> r q m", r=4)[r][:, c0:c1].bitcast(I32),
                    in_=page_plane[r:P:32, c0:c1].bitcast(I32),
                )

        def settle(half, grouped):
            xc = slice(half * BANK, (half + 1) * BANK)
            nc.vector.quantize_mx(
                out=x_codes[:, xc].bitcast(FP8X4),
                scales=x_plane[:, xc],
                in_=grouped[:].rearrange("p c j -> p (c j)"),
            )
            for n in range(N // P):
                rows = slice(n * P, (n + 1) * P)
                acc = bank(3 * half + n, "y_bank")
                nc.tensor.matmul_mx(
                    out=acc[:],
                    lhsT=w2_codes[:, rows].bitcast(FP8X4),
                    lhsT_scale=w2_plane[:, rows],
                    rhs=x_codes[:, xc].bitcast(FP8X4),
                    rhs_scale=x_plane[:, xc],
                    start=True,
                    stop=True,
                )
                y = small([P, BANK], F32, "y")
                nc.scalar.copy(out=y[:], in_=acc[:])
                nc.sync.dma_start(out=out_0[rows, xc], in_=y[:])

        x_grouped = [small([P, BANK, PACK], BF16, "x_grouped") for half in range(2)]
        weave(x_pairs[0], 0, BANK, x_grouped[0])
        weave(x_pairs[1], 0, BANK, x_grouped[1])
        settle(0, x_grouped[0])
        first = large([P, T2 // 2, PACK], BF16, "page_grouped")
        weave(page_pairs[0], 0, T2 // 2, first)
        settle(1, x_grouped[1])
        page_quantise(first, 0, 1024)
        rest = [medium([P, T2 // 4, PACK], BF16, "page_grouped") for part in range(2)]
        for part in range(2):
            weave(page_pairs[1], part * 512, (part + 1) * 512, rest[part])
        for part in range(2):
            page_quantise(rest[part], 1024 + part * 512, 1024 + (part + 1) * 512)
        store_scales(0, T2)
